import numpy as np
import ml_dtypes


def mxq(x, axis, fmt="e4m3"):
    dtype, down = {"e4m3": (ml_dtypes.float8_e4m3fn, 7), "e5m2": (ml_dtypes.float8_e5m2, 14)}[fmt]
    v = np.moveaxis(np.asarray(x, np.float32).astype(ml_dtypes.bfloat16).astype(np.float64), axis, -1)
    blocks = v.reshape(v.shape[:-1] + (-1, 32))
    amax = np.abs(blocks).max(-1, keepdims=True)
    byte = np.maximum(np.where(amax > 0, np.frexp(amax)[1] - 1 + 127, 0) - down, 1)
    scale = np.exp2(byte - 127.0)
    codes = (blocks / scale).astype(np.float32).astype(dtype).astype(np.float64)
    return np.moveaxis((codes * scale).reshape(v.shape), -1, axis)


WIDE = False


def mx_kscale(k):
    if not WIDE:
        return np.ones(k)
    levels = np.array([10, -10, 5, -5, 0])
    if k % 512:
        return np.exp2(np.random.permutation(np.resize(levels, k // 32))).repeat(32)
    a = np.empty((k // 512, 16))
    for p in range(k // 512):
        a[p, :8] = np.random.permutation(np.resize(levels, 8))
        for g in range(8):
            far = levels[np.abs(levels - a[p, g]) >= 10]
            a[p, g + 8] = far[np.random.randint(len(far))]
    return np.exp2(a.ravel()).repeat(32)


def f64(x):
    return np.asarray(x).astype(np.float64)


def striped(idx):
    return np.tile(np.asarray(idx).reshape(-1, 16).T, (8, 1)).astype(np.uint16)


def unstriped(offs):
    return offs[:16].T.reshape(-1).astype(np.int64)


E2M1 = np.array([0.0, 0.5, 1.0, 1.5, 2.0, 3.0, 4.0, 6.0, -0.0, -0.5, -1.0, -1.5, -2.0, -3.0, -4.0, -6.0])


def pack_weight(w, fmt):
    k, n = w.shape
    w = f64(np.asarray(w, np.float32).astype(ml_dtypes.bfloat16)).reshape(k // 32, 32, n)
    amax = np.abs(w).max(1)
    if fmt == "e4m3":
        byte = np.frexp(amax)[1] - 1 + 127 - 7
    else:
        mant, ex = np.frexp(amax / 6.0)
        byte = np.where(mant > 0.5, ex, ex - 1) + 127
    byte = np.clip(np.where(amax > 0, byte, 1), 1, 254)
    scaled = (w * np.exp2(127.0 - byte)[:, None, :]).reshape(k, n).astype(np.float32)
    by_word = np.ascontiguousarray(scaled.reshape(k // 512, 128, 4, n).transpose(0, 1, 3, 2))
    if fmt == "e4m3":
        words = by_word.astype(ml_dtypes.float8_e4m3fn).view(np.uint8)
    else:
        c = by_word.astype(ml_dtypes.float4_e2m1fn).view(np.uint8) & 0xF
        words = (c[..., 0::2] | (c[..., 1::2] << 4)).reshape(k // 512, 128, 2 * n)
    return np.ascontiguousarray(words), np.ascontiguousarray(byte.astype(np.uint8).reshape(k // 512, 16, n))


def unpack_weight(words, scales, fmt):
    g, _, n = scales.shape
    words = np.ascontiguousarray(words).reshape(g, 128, n, -1)
    if fmt == "e4m3":
        vals = words.view(ml_dtypes.float8_e4m3fn).astype(np.float64)
    else:
        nib = np.empty((g, 128, n, 4), np.uint8)
        nib[..., 0::2] = words & 0xF
        nib[..., 1::2] = words >> 4
        vals = E2M1[nib]
    vals = vals * np.repeat(np.exp2(scales.astype(np.float64) - 127.0), 8, axis=1)[..., None]
    return vals.transpose(0, 1, 3, 2).reshape(g * 512, n)


def bf(x):
    return np.asarray(x, np.float32).astype(ml_dtypes.bfloat16)


def planes(Y):
    r, m = Y.shape
    b = f64(bf(Y)).reshape(r // 32, 32, m)
    amax = np.abs(b).max(1)
    byte = np.clip(np.where(amax > 0, np.frexp(amax)[1] - 1 + 127 - 7, 1), 1, 254)
    codes = (b * np.exp2(127.0 - byte)[:, None, :]).reshape(r, m).astype(np.float32).astype(ml_dtypes.float8_e4m3fn).view(np.uint8)
    words = codes.reshape(r // 512, 128, 4, m).transpose(0, 1, 3, 2)
    return np.ascontiguousarray(words), np.ascontiguousarray(byte.astype(np.uint8).reshape(r // 512, 16, m))


D, T, I, U, Q, E = 512, 1024, 512, 2048, 256, 512


def setup_inputs():
    n = np.random.standard_normal
    idx = np.random.permutation(T)[:I]
    idx2 = np.random.permutation(U)[:I]
    fd = mx_kscale(D)
    ft = mx_kscale(T)
    fi = mx_kscale(I)
    ti = np.ones(U)
    ti[idx2] = fi
    cvalsp = pack_weight(n((T, E)) / ft[:, None], "e4m3")
    return {
        "query": (n((D, Q)) * 0.25 / np.sqrt(D) * fd[:, None]).astype(np.float32),
        "keys": (n((D, T)) / fd[:, None]).astype(np.float32),
        "fac": (np.random.uniform(0.5, 2.0, (1, T)) * ft).astype(np.float32),
        "us": (np.random.uniform(0.5, 2.0, (1, I)) * fi).astype(np.float32),
        "cvals_words": cvalsp[0],
        "cvals_scales": cvalsp[1],
        "corr": (n((E, U)) / ti).astype(np.float32),
        "offs": striped(idx),
        "offs2": striped(idx2),
    }


def reference(query, keys, fac, us, cvals_words, cvals_scales, corr, offs, offs2):
    idx = unstriped(offs)
    idx2 = unstriped(offs2)
    cvalsu = unpack_weight(cvals_words, cvals_scales, "e4m3")
    queryq = mxq(f64(query), 0, "e4m3")
    keysq = mxq(f64(keys), 0, "e4m3")
    a = queryq.T @ keysq
    p = np.exp(a - np.max(a, axis=1, keepdims=True))
    w = p / np.sum(p, axis=1, keepdims=True)
    wf = w * f64(fac)
    wt = wf.T
    u1 = w[:, idx] * f64(us)
    ut = u1.T
    ct = f64(corr)[:, idx2].T
    wtq = mxq(wt, 0, "e4m3")
    ctq = mxq(ct, 0, "e4m3")
    utq = mxq(ut, 0, "e4m3")
    o = cvalsu.T @ wtq + ctq.T @ utq
    words, scales = planes(o)
    return o, words, scales

@@ -1,0 +1,380 @@
+from contextlib import ExitStack
+
+import concourse.mybir as mybir
+from concourse.masks import make_identity
+
+D, T, I, U, Q, E = 512, 1024, 512, 2048, 256, 512
+FLOPS = 2 * D * Q * T + 2 * T * E * Q + 2 * I * E * Q
+
+F32 = mybir.dt.float32
+BF16 = mybir.dt.bfloat16
+I32 = mybir.dt.int32
+U32 = mybir.dt.uint32
+U16 = mybir.dt.uint16
+U8 = mybir.dt.uint8
+FP8X4 = mybir.dt.float8_e4m3fn_x4
+ALU = mybir.AluOpType
+ACT = mybir.ActivationFunctionType
+AXIS_X = mybir.AxisListType.X
+
+P = 128
+PACK = 4
+K_PASS = P * PACK
+HALVES = Q // P
+T_PASSES = T // K_PASS
+CHUNK = 256
+CHUNKS = T // CHUNK
+SCALAR_TOKENS = (0, 0, 128, 128)
+SCALAR_QUERIES = 0
+VECTOR_SLOTS = (0, 0, 512, 256)
+OV2 = "p1"
+LAG = 4
+OVER = (None, "q_bf", "k_bf0", "q_bf")
+
+
+def interleave(copy, dst, src):
+    copy(
+        out=dst.rearrange("p (c i) j -> p c j i", i=4),
+        in_=src.rearrange("p j (c i) -> p c j i", i=4),
+    )
+
+
+def tile_attend_valuepatch_pl_kernel(
+    tc, query, keys, fac, us, cvals_words, cvals_scales, corr, offs, offs2, out_0, out_1, out_2
+):
+    nc = tc.nc
+    with ExitStack() as ctx:
+        lists = ctx.enter_context(tc.tile_pool(name="lists", bufs=1))
+        sb = ctx.enter_context(tc.tile_pool(name="sb", bufs=1))
+        psum = ctx.enter_context(tc.psum_pool(name="psum", bufs=1))
+
+        def sbuf(name, shape, dtype, over=None):
+            return sb.tile(shape, dtype, name=name, tag=over or name, align_bytes=64)
+
+        def bank(tag, name, shape):
+            return psum.tile(shape, F32, name=name, tag=tag)
+
+        def quantize(name, grouped, width):
+            codes = sbuf(name + "_codes", [P, width], U32)
+            scales = sbuf(name + "_scales", [P, width], U8)
+            nc.vector.quantize_mx(out=codes[:].bitcast(FP8X4), scales=scales[:], in_=grouped)
+            return codes, scales
+
+        q_raw = sbuf("q_raw", [P, PACK, Q], F32)
+        nc.sync.dma_start(out=q_raw[:], in_=query.rearrange("(p j) q -> p j q", j=PACK))
+        keys_v = keys.rearrange("(p j) t -> p j t", j=PACK)
+        k_raw = []
+        for c in range(CHUNKS):
+            k_raw.append(sbuf("k_raw%d" % c, [P, PACK, CHUNK], F32))
+            nc.sync.dma_start(out=k_raw[c][:], in_=keys_v[:, :, c * CHUNK : (c + 1) * CHUNK])
+        cv_raw = sbuf("cv_raw", [P, T_PASSES, E], U32)
+        nc.sync.dma_start(
+            out=cv_raw[:].bitcast(I32),
+            in_=cvals_words.rearrange("z p e j -> p z (e j)").bitcast(I32),
+        )
+        cs_raw = sbuf("cs_raw", [P, E], U8)
+        nc.gpsimd.memset(cs_raw[:].bitcast(I32), 0)
+        for quad in range(4):
+            nc.sync.dma_start(
+                out=cs_raw[32 * quad : 32 * quad + 4 * T_PASSES, :].bitcast(I32),
+                in_=cvals_scales[:, 4 * quad : 4 * quad + 4, :].bitcast(I32),
+            )
+        fac_col = sbuf("fac_col", [P, T_PASSES, PACK], F32)
+        nc.sync.dma_start(out=fac_col[:], in_=fac[0].rearrange("(z p j) -> p z j", z=T_PASSES, j=PACK))
+        corr_v = corr.rearrange("(p r) u -> p r u", r=PACK)
+        corr_sb = [sbuf("corr%d" % r, [P, U], F32) for r in range(PACK)]
+        nc.sync.dma_start(out=corr_sb[0][:], in_=corr_v[:, 0, :])
+        corr_list = lists.tile([P, I // 16], U16, name="corr_list")
+        nc.sync.dma_start(corr_list[:], offs2)
+        w_list = lists.tile([P, I // 16], U16, name="w_list")
+        nc.sync.dma_start(w_list[:], offs)
+        us_col = sbuf("us_col", [P, PACK], F32)
+        nc.sync.dma_start(out=us_col[:], in_=us[0].rearrange("(p j) -> p j", j=PACK))
+        for r in range(1, PACK):
+            nc.sync.dma_start(out=corr_sb[r][:], in_=corr_v[:, r, :])
+
+        ident = sbuf("ident", [P, P], F32)
+        make_identity(nc, ident[:])
+
+        def shared_interleave(dst, src, split):
+            if split > 0:
+                interleave(nc.scalar.copy, dst[:, :split, :], src[:, :, :split])
+            if split < dst.shape[1]:
+                interleave(nc.vector.tensor_copy, dst[:, split:, :], src[:, :, split:])
+
+        q_bf = sbuf("q_bf", [P, Q, PACK], BF16)
+        shared_interleave(q_bf, q_raw, SCALAR_QUERIES)
+        q_codes, q_scales = quantize("q", q_bf[:].rearrange("p q j -> p (q j)"), Q)
+
+        neg_max = sbuf("neg_max", [P, HALVES, CHUNKS], F32)
+        chunk_sum = sbuf("chunk_sum", [P, HALVES, CHUNKS], F32)
+        p_sb = [sbuf("p%d" % h, [P, T], F32) for h in range(HALVES)]
+        scores = [None] * CHUNKS
+
+        def score(c):
+            k_bf = sbuf("k_bf%d" % c, [P, CHUNK, PACK], BF16, over=OVER[c])
+            shared_interleave(k_bf, k_raw[c], SCALAR_TOKENS[c])
+            k_codes, k_scales = quantize("k%d" % c, k_bf[:].rearrange("p t j -> p (t j)"), CHUNK)
+            scores[c] = bank("b%d" % c, "scores%d" % c, [P, HALVES, CHUNK])
+            for h in range(HALVES):
+                nc.tensor.matmul_mx(
+                    out=scores[c][:, h, :],
+                    lhsT=q_codes[:, h * P : (h + 1) * P].bitcast(FP8X4),
+                    lhsT_scale=q_scales[:, h * P : (h + 1) * P],
+                    rhs=k_codes[:].bitcast(FP8X4),
+                    rhs_scale=k_scales[:],
+                    start=True,
+                    stop=True,
+                )
+
+        def exponentiate(c):
+            nc.vector.tensor_reduce(
+                out=neg_max[:, :, c], in_=scores[c][:], axis=AXIS_X, op=ALU.max, negate=True
+            )
+            for h in range(HALVES):
+                nc.scalar.activation(
+                    out=p_sb[h][:, c * CHUNK : (c + 1) * CHUNK],
+                    in_=scores[c][:, h, :],
+                    func=ACT.Exp,
+                    bias=neg_max[:, h, c : c + 1],
+                    accum_out=chunk_sum[:, h, c : c + 1],
+                )
+
+        for c in range(CHUNKS + LAG):
+            if c < CHUNKS:
+                score(c)
+            if c >= LAG:
+                exponentiate(c - LAG)
+
+        fac_row = []
+        for z in range(T_PASSES):
+            fac_row.append(bank("b%d" % (2 + z), "fac_row%d" % z, [P, PACK, P]))
+            for j in range(PACK):
+                nc.tensor.transpose(fac_row[z][:, j, :], fac_col[:, z, j : j + 1].to_broadcast([P, P]), ident[:])
+
+        neg_row_max = sbuf("neg_row_max", [P, HALVES], F32)
+        nc.vector.tensor_reduce(out=neg_row_max[:], in_=neg_max[:], axis=AXIS_X, op=ALU.min)
+        rescale = sbuf("rescale", [P, HALVES, CHUNKS], F32)
+        for h in range(HALVES):
+            nc.scalar.activation(
+                out=rescale[:, h, :], in_=neg_max[:, h, :], func=ACT.Exp, scale=-1.0, bias=neg_row_max[:, h : h + 1]
+            )
+
+        cv_codes = sbuf("cv_codes", [P, T_PASSES, E], U32, over="k%d_codes" % (CHUNKS - 1))
+        cv_scales = sbuf("cv_scales", [P, E], U8, over="k%d_scales" % (CHUNKS - 1))
+        nc.vector.tensor_copy(
+            out=cv_codes[:].bitcast(I32).rearrange("p z (r m) -> p z m r", r=PACK),
+            in_=cv_raw[:].bitcast(I32).rearrange("p z (m r) -> p z m r", r=PACK),
+        )
+        nc.vector.tensor_copy(
+            out=cv_scales[:].rearrange("p (r m) -> p m r", r=PACK),
+            in_=cs_raw[:].rearrange("p (m r) -> p m r", r=PACK),
+        )
+
+        w_sb, wf_bf, inv_sum = [None] * HALVES, [None] * HALVES, [None] * HALVES
+
+        def row_sum(h):
+            terms = sbuf("terms%d" % h, [P, CHUNKS], F32)
+            total = sbuf("total%d" % h, [P, 1], F32)
+            nc.vector.scalar_tensor_tensor(
+                out=terms[:],
+                in0=chunk_sum[:, h, :],
+                scalar=1.0,
+                in1=rescale[:, h, :],
+                op0=ALU.mult,
+                op1=ALU.mult,
+                accum_out=total[:],
+            )
+            inv_sum[h] = sbuf("inv_sum%d" % h, [P, 1], F32)
+            nc.vector.reciprocal(out=inv_sum[h][:], in_=total[:])
+
+        out_ps = [None, None]
+        ut_q = [None, None]
+        ct_q = [None] * PACK
+
+        def normalise(h):
+            w_sb[h] = sbuf("w%d" % h, [P, T], F32)
+            for c in range(CHUNKS):
+                cols = slice(c * CHUNK, (c + 1) * CHUNK)
+                nc.vector.tensor_scalar(
+                    out=w_sb[h][:, cols],
+                    in0=p_sb[h][:, cols],
+                    scalar1=rescale[:, h, c : c + 1],
+                    scalar2=inv_sum[h][:],
+                    op0=ALU.mult,
+                    op1=ALU.mult,
+                )
+
+        def weigh(h):
+            wf_bf[h] = sbuf("wf%d" % h, [P, T], BF16)
+            for z in range(T_PASSES):
+                cols = slice(z * K_PASS, (z + 1) * K_PASS)
+                nc.vector.tensor_tensor(
+                    out=wf_bf[h][:, cols].rearrange("p (s j) -> p s j", j=PACK),
+                    in0=w_sb[h][:, cols].rearrange("p (s j) -> p s j", j=PACK),
+                    in1=fac_row[z][:].rearrange("p j s -> p s j"),
+                    op=ALU.mult,
+                )
+
+        def gather_w(h):
+            picked = sbuf("picked%d" % h, [P, I], F32)
+            nc.scalar.activation(out=picked[:], in_=w_sb[h][:].indirect(w_list[:]), func=ACT.Copy)
+            return picked
+
+        wt_bf = [None] * HALVES
+        wt_ps = [None] * HALVES
+
+        def turn_weights(h):
+            turned = bank("x%d" % h, "wt_ps%d" % h, [P, T_PASSES, 2, P])
+            words = wf_bf[h][:].bitcast(F32)
+            for z in range(T_PASSES):
+                for u in range(2):
+                    nc.tensor.transpose(
+                        turned[:, z, u, :], words[:, 256 * z + u : 256 * (z + 1) : 2], ident[:]
+                    )
+            wt_ps[h] = turned
+
+        def copy_weights(h):
+            turned = wt_ps[h]
+            wt_bf[h] = sbuf("wt_bf%d" % h, [P, T_PASSES * P * PACK], BF16)
+            nc.scalar.copy(
+                out=wt_bf[h][:].bitcast(F32).rearrange("p (z q u) -> p z q u", z=T_PASSES, u=2),
+                in_=turned[:].rearrange("p z u q -> p z q u"),
+            )
+
+        def coarse(h):
+            wt_codes, wt_scales = quantize("wt%d" % h, wt_bf[h][:], T_PASSES * P)
+            out_ps[h] = bank("b%d" % h, "out_ps%d" % h, [P, PACK, P])
+            for z in range(T_PASSES):
+                for r in range(PACK):
+                    nc.tensor.matmul_mx(
+                        out=out_ps[h][:, r, :],
+                        lhsT=cv_codes[:, z, r * P : (r + 1) * P].bitcast(FP8X4),
+                        lhsT_scale=cv_scales[4 * z :, r * P : (r + 1) * P],
+                        rhs=wt_codes[:, z * P : (z + 1) * P].bitcast(FP8X4),
+                        rhs_scale=wt_scales[:, z * P : (z + 1) * P],
+                        start=(z == 0 and r == 0),
+                        stop=False,
+                    )
+
+        ut_ps = [None] * HALVES
+
+        def turn_listed(h, picked):
+            turned = bank("x%d" % h, "ut_ps%d" % h, [P, PACK, P])
+            for j in range(PACK):
+                nc.tensor.transpose(turned[:, j, :], picked[:, j::PACK], ident[:])
+            ut_ps[h] = turned
+
+        def listed(h):
+            turned = ut_ps[h]
+            ut_bf = sbuf("ut_bf%d" % h, [P, P, PACK], BF16)
+            nc.vector.tensor_tensor(
+                out=ut_bf[:],
+                in0=turned[:].rearrange("p j q -> p q j"),
+                in1=us_col[:].unsqueeze(1).to_broadcast([P, P, PACK]),
+                op=ALU.mult,
+            )
+            ut_q[h] = quantize("ut%d" % h, ut_bf[:].rearrange("p q j -> p (q j)"), P)
+
+        ct_bf = [None] * PACK
+        corr_rows = [None] * PACK
+
+        def gather_corr(r, vector_share, rows):
+            cut = I - vector_share
+            if cut:
+                nc.scalar.activation(
+                    out=rows[:, :cut], in_=corr_sb[r][:].indirect(corr_list[:, : cut // 16]), func=ACT.Copy
+                )
+            if vector_share:
+                nc.vector.tensor_copy(out=rows[:, cut:], in_=corr_sb[r][:].indirect(corr_list[:, cut // 16 :]))
+            corr_rows[r] = rows
+
+        def turn_corr(r, grouped):
+            turned = bank("f%d" % (r % 2), "ct_ps%d" % r, [P, 2, P])
+            words = corr_rows[r].bitcast(F32)
+            for u in range(2):
+                nc.tensor.transpose(turned[:, u, :], words[:, u::2], ident[:])
+            ct_bf[r] = grouped
+            nc.scalar.copy(
+                out=ct_bf[r].bitcast(F32).rearrange("p (m u) -> p m u", u=2),
+                in_=turned[:].rearrange("p u m -> p m u"),
+            )
+
+        def quantize_corr(r):
+            ct_q[r] = quantize("ct%d" % r, ct_bf[r], P)
+
+        def patch(r, h):
+            nc.tensor.matmul_mx(
+                out=out_ps[h][:, r, :],
+                lhsT=ct_q[r][0][:].bitcast(FP8X4),
+                lhsT_scale=ct_q[r][1][:],
+                rhs=ut_q[h][0][:].bitcast(FP8X4),
+                rhs_scale=ut_q[h][1][:],
+                start=False,
+                stop=(r == PACK - 1),
+            )
+
+        row_sum(0)
+        gather_corr(0, VECTOR_SLOTS[0], sbuf("rows0", [P, I], BF16, over="neg_max")[:])
+        normalise(0)
+        row_sum(1)
+        picked0 = gather_w(0)
+        weigh(0)
+        turn_corr(0, sbuf("ct_bf0", [P, I], BF16, over="p0")[:])
+        turn_weights(0)
+        copy_weights(0)
+        turn_listed(0, picked0)
+        gather_corr(1, VECTOR_SLOTS[1], sbuf("rows1", [P, I], BF16, over="wf0")[:])
+        normalise(1)
+        picked1 = gather_w(1)
+        weigh(1)
+        turn_weights(1)
+        copy_weights(1)
+        coarse(0)
+        listed(0)
+        quantize_corr(0)
+        patch(0, 0)
+        turn_listed(1, picked1)
+        turn_corr(1, sbuf("ct_bf1", [P, I], BF16)[:])
+        gather_corr(2, VECTOR_SLOTS[2], sbuf("rows2", [P, I], BF16, over=OV2)[:])
+        coarse(1)
+        gather_corr(3, VECTOR_SLOTS[3], sbuf("rows3", [P, I], BF16, over="wf1")[:])
+        listed(1)
+        turn_corr(2, sbuf("ct_bf2", [P, I], BF16)[:])
+        quantize_corr(1)
+        patch(1, 0)
+        patch(0, 1)
+        patch(1, 1)
+        turn_corr(3, sbuf("ct_bf3", [P, I], BF16)[:])
+        quantize_corr(2)
+        quantize_corr(3)
+        for r in (2, 3):
+            for h in range(HALVES):
+                patch(r, h)
+
+        out_v = out_0.rearrange("(p r) q -> p r q", r=PACK)
+        o_sb = [sbuf("o_sb%d" % h, [P, PACK, P], F32) for h in range(HALVES)]
+        o_bf = [sbuf("o_bf%d" % h, [P, P, PACK], BF16) for h in range(HALVES)]
+        o_codes = sbuf("o_codes", [P, Q], U32)
+        o_scales = sbuf("o_scales", [P, Q], U8)
+        nc.vector.tensor_copy(out=o_bf[0][:], in_=out_ps[0][:].rearrange("p r q -> p q r"))
+        nc.scalar.copy(out=o_sb[1][:], in_=out_ps[1][:])
+        nc.sync.dma_start(out=out_v[:, :, P:], in_=o_sb[1][:])
+        nc.scalar.copy(out=o_sb[0][:], in_=out_ps[0][:])
+        nc.sync.dma_start(out=out_v[:, :, :P], in_=o_sb[0][:])
+        interleave(nc.vector.tensor_copy, o_bf[1][:], o_sb[1][:])
+        for h in range(HALVES):
+            nc.vector.quantize_mx(
+                out=o_codes[:, h * P : (h + 1) * P].bitcast(FP8X4),
+                scales=o_scales[:, h * P : (h + 1) * P],
+                in_=o_bf[h][:].rearrange("p q r -> p (q r)"),
+            )
+        nc.sync.dma_start(
+            out=out_1[0].rearrange("p q j -> p (q j)").bitcast(I32), in_=o_codes[:].bitcast(I32)
+        )
+        for quad in range(4):
+            queue = nc.scalar if quad % 2 else nc.sync
+            queue.dma_start(
+                out=out_2[0][4 * quad : 4 * quad + 4, :].bitcast(I32),
+                in_=o_scales[32 * quad : 32 * quad + 4, :].bitcast(I32),
+            )

@@ -25,9 +25,16 @@ T_PASSES = T // K_PASS
 CHUNK = 256
 CHUNKS = T // CHUNK
 SCALAR_TOKENS = (0, 0, 128, 128)
-SCALAR_QUERIES = 0
-VECTOR_SLOTS = (0, 0, 512, 256)
-OV2 = "p1"
+SCALAR_QUERIES = 128
+VECTOR_SLOTS = (0, 0, 512, 0)
+OVM = "k_raw2"
+OVA = "wf0"
+OVB = "w0"
+OVC = "corr1"
+OVD = "wf1"
+OVE = "corr2"
+OVF = "corr1"
+UTB = ("f1", "b3")
 LAG = 4
 OVER = (None, "q_bf", "k_bf0", "q_bf")
 
@@ -54,8 +61,8 @@ def tile_attend_valuepatch_pl_kernel(
         def bank(tag, name, shape):
             return psum.tile(shape, F32, name=name, tag=tag)
 
-        def quantize(name, grouped, width):
-            codes = sbuf(name + "_codes", [P, width], U32)
+        def quantize(name, grouped, width, over=None):
+            codes = sbuf(name + "_codes", [P, width], U32, over=over)
             scales = sbuf(name + "_scales", [P, width], U8)
             nc.vector.quantize_mx(out=codes[:].bitcast(FP8X4), scales=scales[:], in_=grouped)
             return codes, scales
@@ -75,7 +82,7 @@ def tile_attend_valuepatch_pl_kernel(
         cs_raw = sbuf("cs_raw", [P, E], U8)
         nc.gpsimd.memset(cs_raw[:].bitcast(I32), 0)
         for quad in range(4):
-            nc.sync.dma_start(
+            nc.scalar.dma_start(
                 out=cs_raw[32 * quad : 32 * quad + 4 * T_PASSES, :].bitcast(I32),
                 in_=cvals_scales[:, 4 * quad : 4 * quad + 4, :].bitcast(I32),
             )
@@ -93,6 +100,7 @@ def tile_attend_valuepatch_pl_kernel(
         for r in range(1, PACK):
             nc.sync.dma_start(out=corr_sb[r][:], in_=corr_v[:, r, :])
 
+
         ident = sbuf("ident", [P, P], F32)
         make_identity(nc, ident[:])
 
@@ -106,7 +114,7 @@ def tile_attend_valuepatch_pl_kernel(
         shared_interleave(q_bf, q_raw, SCALAR_QUERIES)
         q_codes, q_scales = quantize("q", q_bf[:].rearrange("p q j -> p (q j)"), Q)
 
-        neg_max = sbuf("neg_max", [P, HALVES, CHUNKS], F32)
+        neg_max = sbuf("neg_max", [P, HALVES, CHUNKS], F32, over=OVM)
         chunk_sum = sbuf("chunk_sum", [P, HALVES, CHUNKS], F32)
         p_sb = [sbuf("p%d" % h, [P, T], F32) for h in range(HALVES)]
         scores = [None] * CHUNKS
@@ -216,9 +224,8 @@ def tile_attend_valuepatch_pl_kernel(
                     op=ALU.mult,
                 )
 
-        def gather_w(h):
-            picked = sbuf("picked%d" % h, [P, I], F32)
-            nc.scalar.activation(out=picked[:], in_=w_sb[h][:].indirect(w_list[:]), func=ACT.Copy)
+        def gather_w(h, picked):
+            nc.scalar.activation(out=picked, in_=w_sb[h][:].indirect(w_list[:]), func=ACT.Copy)
             return picked
 
         wt_bf = [None] * HALVES
@@ -234,16 +241,16 @@ def tile_attend_valuepatch_pl_kernel(
                     )
             wt_ps[h] = turned
 
-        def copy_weights(h):
+        def copy_weights(h, grouped):
             turned = wt_ps[h]
-            wt_bf[h] = sbuf("wt_bf%d" % h, [P, T_PASSES * P * PACK], BF16)
+            wt_bf[h] = grouped
             nc.scalar.copy(
-                out=wt_bf[h][:].bitcast(F32).rearrange("p (z q u) -> p z q u", z=T_PASSES, u=2),
+                out=wt_bf[h].bitcast(F32).rearrange("p (z q u) -> p z q u", z=T_PASSES, u=2),
                 in_=turned[:].rearrange("p z u q -> p z q u"),
             )
 
-        def coarse(h):
-            wt_codes, wt_scales = quantize("wt%d" % h, wt_bf[h][:], T_PASSES * P)
+        def coarse(h, over=None):
+            wt_codes, wt_scales = quantize("wt%d" % h, wt_bf[h], T_PASSES * P, over)
             out_ps[h] = bank("b%d" % h, "out_ps%d" % h, [P, PACK, P])
             for z in range(T_PASSES):
                 for r in range(PACK):
@@ -260,14 +267,14 @@ def tile_attend_valuepatch_pl_kernel(
         ut_ps = [None] * HALVES
 
         def turn_listed(h, picked):
-            turned = bank("x%d" % h, "ut_ps%d" % h, [P, PACK, P])
+            turned = bank(UTB[h], "ut_ps%d" % h, [P, PACK, P])
             for j in range(PACK):
                 nc.tensor.transpose(turned[:, j, :], picked[:, j::PACK], ident[:])
             ut_ps[h] = turned
 
-        def listed(h):
+        def listed(h, over=None):
             turned = ut_ps[h]
-            ut_bf = sbuf("ut_bf%d" % h, [P, P, PACK], BF16)
+            ut_bf = sbuf("ut_bf%d" % h, [P, P, PACK], BF16, over=over)
             nc.vector.tensor_tensor(
                 out=ut_bf[:],
                 in0=turned[:].rearrange("p j q -> p q j"),
@@ -290,7 +297,7 @@ def tile_attend_valuepatch_pl_kernel(
             corr_rows[r] = rows
 
         def turn_corr(r, grouped):
-            turned = bank("f%d" % (r % 2), "ct_ps%d" % r, [P, 2, P])
+            turned = bank(("f0", "x0", "f0", "b2")[r], "ct_ps%d" % r, [P, 2, P])
             words = corr_rows[r].bitcast(F32)
             for u in range(2):
                 nc.tensor.transpose(turned[:, u, :], words[:, u::2], ident[:])
@@ -315,40 +322,37 @@ def tile_attend_valuepatch_pl_kernel(
             )
 
         row_sum(0)
-        gather_corr(0, VECTOR_SLOTS[0], sbuf("rows0", [P, I], BF16, over="neg_max")[:])
+        gather_corr(0, VECTOR_SLOTS[0], sbuf("rows0", [P, I], BF16, over=OVM or "neg_max")[:])
         normalise(0)
         row_sum(1)
-        picked0 = gather_w(0)
+        picked0 = gather_w(0, sbuf("picked0", [P, I], F32, over="corr0")[:])
         weigh(0)
         turn_corr(0, sbuf("ct_bf0", [P, I], BF16, over="p0")[:])
         turn_weights(0)
-        copy_weights(0)
+        copy_weights(0, sbuf("wt_bf0", [P, T], BF16)[:])
         turn_listed(0, picked0)
-        gather_corr(1, VECTOR_SLOTS[1], sbuf("rows1", [P, I], BF16, over="wf0")[:])
         normalise(1)
-        picked1 = gather_w(1)
+        picked1 = gather_w(1, sbuf("picked1", [P, I], F32, over=OVA)[:])
+        gather_corr(1, VECTOR_SLOTS[1], sbuf("rows1", [P, I], BF16, over=OVB)[:])
         weigh(1)
         turn_weights(1)
-        copy_weights(1)
+        copy_weights(1, sbuf("wt_bf1", [P, T], BF16, over=OVC)[:])
         coarse(0)
         listed(0)
         quantize_corr(0)
         patch(0, 0)
         turn_listed(1, picked1)
-        turn_corr(1, sbuf("ct_bf1", [P, I], BF16)[:])
-        gather_corr(2, VECTOR_SLOTS[2], sbuf("rows2", [P, I], BF16, over=OV2)[:])
-        coarse(1)
-        gather_corr(3, VECTOR_SLOTS[3], sbuf("rows3", [P, I], BF16, over="wf1")[:])
-        listed(1)
-        turn_corr(2, sbuf("ct_bf2", [P, I], BF16)[:])
-        quantize_corr(1)
-        patch(1, 0)
-        patch(0, 1)
-        patch(1, 1)
+        gather_corr(2, VECTOR_SLOTS[2], sbuf("rows2", [P, I], BF16, over="ut_bf0")[:])
+        gather_corr(3, VECTOR_SLOTS[3], sbuf("rows3", [P, I], BF16, over=OVD)[:])
+        after_corr3 = sbuf("after_corr3", [P, 2 * I], BF16, over="corr3")
+        turn_corr(1, after_corr3[:, :I])
+        turn_corr(2, after_corr3[:, I:])
         turn_corr(3, sbuf("ct_bf3", [P, I], BF16)[:])
-        quantize_corr(2)
-        quantize_corr(3)
-        for r in (2, 3):
+        coarse(1, OVE)
+        listed(1, OVF)
+        patch(0, 1)
+        for r in range(1, PACK):
+            quantize_corr(r)
             for h in range(HALVES):
                 patch(r, h)
 

@@ -25,9 +25,10 @@ T_PASSES = T // K_PASS
 CHUNK = 256
 CHUNKS = T // CHUNK
 SCALAR_TOKENS = (0, 0, 128, 128)
-SCALAR_QUERIES = 128
-VECTOR_SLOTS = (0, 0, 512, 0)
+SCALAR_QUERIES = 0
+VECTOR_SLOTS = (0, 0, 512, 128)
 OVM = "k_raw2"
+OV2 = "wf0"
 OVA = "wf0"
 OVB = "w0"
 OVC = "corr1"
@@ -35,8 +36,10 @@ OVD = "wf1"
 OVE = "corr2"
 OVF = "corr1"
 UTB = ("f1", "b3")
+CTB = ("f0", "x0", "f0", "x1")
+ENG = (1, 0, 1, 0)
 LAG = 4
-OVER = (None, "q_bf", "k_bf0", "q_bf")
+OVER = (None, None, None, None)
 
 
 def interleave(copy, dst, src):
@@ -61,8 +64,9 @@ def tile_attend_valuepatch_pl_kernel(
         def bank(tag, name, shape):
             return psum.tile(shape, F32, name=name, tag=tag)
 
-        def quantize(name, grouped, width, over=None):
-            codes = sbuf(name + "_codes", [P, width], U32, over=over)
+        def quantize(name, grouped, width, codes=None):
+            if codes is None:
+                codes = sbuf(name + "_codes", [P, width], U32)
             scales = sbuf(name + "_scales", [P, width], U8)
             nc.vector.quantize_mx(out=codes[:].bitcast(FP8X4), scales=scales[:], in_=grouped)
             return codes, scales
@@ -87,7 +91,7 @@ def tile_attend_valuepatch_pl_kernel(
                 in_=cvals_scales[:, 4 * quad : 4 * quad + 4, :].bitcast(I32),
             )
         fac_col = sbuf("fac_col", [P, T_PASSES, PACK], F32)
-        nc.sync.dma_start(out=fac_col[:], in_=fac[0].rearrange("(z p j) -> p z j", z=T_PASSES, j=PACK))
+        nc.scalar.dma_start(out=fac_col[:], in_=fac[0].rearrange("(z p j) -> p z j", z=T_PASSES, j=PACK))
         corr_v = corr.rearrange("(p r) u -> p r u", r=PACK)
         corr_sb = [sbuf("corr%d" % r, [P, U], F32) for r in range(PACK)]
         nc.sync.dma_start(out=corr_sb[0][:], in_=corr_v[:, 0, :])
@@ -96,7 +100,7 @@ def tile_attend_valuepatch_pl_kernel(
         w_list = lists.tile([P, I // 16], U16, name="w_list")
         nc.sync.dma_start(w_list[:], offs)
         us_col = sbuf("us_col", [P, PACK], F32)
-        nc.sync.dma_start(out=us_col[:], in_=us[0].rearrange("(p j) -> p j", j=PACK))
+        nc.scalar.dma_start(out=us_col[:], in_=us[0].rearrange("(p j) -> p j", j=PACK))
         for r in range(1, PACK):
             nc.sync.dma_start(out=corr_sb[r][:], in_=corr_v[:, r, :])
 
@@ -116,6 +120,8 @@ def tile_attend_valuepatch_pl_kernel(
 
         neg_max = sbuf("neg_max", [P, HALVES, CHUNKS], F32, over=OVM)
         chunk_sum = sbuf("chunk_sum", [P, HALVES, CHUNKS], F32)
+        neg_row_max = sbuf("neg_row_max", [P, HALVES], F32)
+        rescale = sbuf("rescale", [P, HALVES, CHUNKS], F32)
         p_sb = [sbuf("p%d" % h, [P, T], F32) for h in range(HALVES)]
         scores = [None] * CHUNKS
 
@@ -139,6 +145,8 @@ def tile_attend_valuepatch_pl_kernel(
             nc.vector.tensor_reduce(
                 out=neg_max[:, :, c], in_=scores[c][:], axis=AXIS_X, op=ALU.max, negate=True
             )
+            if c == CHUNKS - 1:
+                nc.vector.tensor_reduce(out=neg_row_max[:], in_=neg_max[:], axis=AXIS_X, op=ALU.min)
             for h in range(HALVES):
                 nc.scalar.activation(
                     out=p_sb[h][:, c * CHUNK : (c + 1) * CHUNK],
@@ -147,6 +155,14 @@ def tile_attend_valuepatch_pl_kernel(
                     bias=neg_max[:, h, c : c + 1],
                     accum_out=chunk_sum[:, h, c : c + 1],
                 )
+                if c == CHUNKS - 1:
+                    nc.scalar.activation(
+                        out=rescale[:, h, :],
+                        in_=neg_max[:, h, :],
+                        func=ACT.Exp,
+                        scale=-1.0,
+                        bias=neg_row_max[:, h : h + 1],
+                    )
 
         for c in range(CHUNKS + LAG):
             if c < CHUNKS:
@@ -154,29 +170,25 @@ def tile_attend_valuepatch_pl_kernel(
             if c >= LAG:
                 exponentiate(c - LAG)
 
+        us_row = bank("b1", "us_row", [P, PACK, P])
+        for j in range(PACK):
+            nc.tensor.transpose(us_row[:, j, :], us_col[:, j : j + 1].to_broadcast([P, P]), ident[:])
         fac_row = []
         for z in range(T_PASSES):
             fac_row.append(bank("b%d" % (2 + z), "fac_row%d" % z, [P, PACK, P]))
             for j in range(PACK):
                 nc.tensor.transpose(fac_row[z][:, j, :], fac_col[:, z, j : j + 1].to_broadcast([P, P]), ident[:])
 
-        neg_row_max = sbuf("neg_row_max", [P, HALVES], F32)
-        nc.vector.tensor_reduce(out=neg_row_max[:], in_=neg_max[:], axis=AXIS_X, op=ALU.min)
-        rescale = sbuf("rescale", [P, HALVES, CHUNKS], F32)
-        for h in range(HALVES):
-            nc.scalar.activation(
-                out=rescale[:, h, :], in_=neg_max[:, h, :], func=ACT.Exp, scale=-1.0, bias=neg_row_max[:, h : h + 1]
-            )
 
-        cv_codes = sbuf("cv_codes", [P, T_PASSES, E], U32, over="k%d_codes" % (CHUNKS - 1))
+        cv_codes = sbuf("cv_codes", [P, T_PASSES, E], U32, over="k_bf%d" % (CHUNKS - 1))
         cv_scales = sbuf("cv_scales", [P, E], U8, over="k%d_scales" % (CHUNKS - 1))
         nc.vector.tensor_copy(
-            out=cv_codes[:].bitcast(I32).rearrange("p z (r m) -> p z m r", r=PACK),
-            in_=cv_raw[:].bitcast(I32).rearrange("p z (m r) -> p z m r", r=PACK),
+            out=cv_codes[:].bitcast(I32).rearrange("p z (r c i) -> p z c r i", r=PACK, i=4),
+            in_=cv_raw[:].bitcast(I32).rearrange("p z (c i r) -> p z c r i", r=PACK, i=4),
         )
         nc.vector.tensor_copy(
-            out=cv_scales[:].rearrange("p (r m) -> p m r", r=PACK),
-            in_=cs_raw[:].rearrange("p (m r) -> p m r", r=PACK),
+            out=cv_scales[:].rearrange("p (r c i) -> p c r i", r=PACK, i=16),
+            in_=cs_raw[:].rearrange("p (c i r) -> p c r i", r=PACK, i=16),
         )
 
         w_sb, wf_bf, inv_sum = [None] * HALVES, [None] * HALVES, [None] * HALVES
@@ -249,9 +261,9 @@ def tile_attend_valuepatch_pl_kernel(
                 in_=turned[:].rearrange("p z u q -> p z q u"),
             )
 
-        def coarse(h, over=None):
-            wt_codes, wt_scales = quantize("wt%d" % h, wt_bf[h], T_PASSES * P, over)
-            out_ps[h] = bank("b%d" % h, "out_ps%d" % h, [P, PACK, P])
+        def coarse(h, codes=None):
+            wt_codes, wt_scales = quantize("wt%d" % h, wt_bf[h], T_PASSES * P, codes)
+            out_ps[h] = bank(("b0", "b2")[h], "out_ps%d" % h, [P, PACK, P])
             for z in range(T_PASSES):
                 for r in range(PACK):
                     nc.tensor.matmul_mx(
@@ -264,24 +276,34 @@ def tile_attend_valuepatch_pl_kernel(
                         stop=False,
                     )
 
-        ut_ps = [None] * HALVES
+        ul_bf = [None] * HALVES
+        ut_bf = [None] * HALVES
 
-        def turn_listed(h, picked):
-            turned = bank(UTB[h], "ut_ps%d" % h, [P, PACK, P])
-            for j in range(PACK):
-                nc.tensor.transpose(turned[:, j, :], picked[:, j::PACK], ident[:])
-            ut_ps[h] = turned
-
-        def listed(h, over=None):
-            turned = ut_ps[h]
-            ut_bf = sbuf("ut_bf%d" % h, [P, P, PACK], BF16, over=over)
+        def weigh_listed(h, picked):
+            ul_bf[h] = sbuf("ul%d" % h, [P, I], BF16)
             nc.vector.tensor_tensor(
-                out=ut_bf[:],
-                in0=turned[:].rearrange("p j q -> p q j"),
-                in1=us_col[:].unsqueeze(1).to_broadcast([P, P, PACK]),
+                out=ul_bf[h][:].rearrange("p (s j) -> p s j", j=PACK),
+                in0=picked.rearrange("p (s j) -> p s j", j=PACK),
+                in1=us_row[:].rearrange("p j s -> p s j"),
                 op=ALU.mult,
             )
-            ut_q[h] = quantize("ut%d" % h, ut_bf[:].rearrange("p q j -> p (q j)"), P)
+
+        def turn_pass(rows, tag, name, grouped, copy):
+            turned = bank(tag, name, [P, 2, P])
+            words = rows.bitcast(F32)
+            for u in range(2):
+                nc.tensor.transpose(turned[:, u, :], words[:, u::2], ident[:])
+            copy(
+                out=grouped.bitcast(F32).rearrange("p (m u) -> p m u", u=2),
+                in_=turned[:].rearrange("p u m -> p m u"),
+            )
+
+        def turn_listed(h, grouped, copy):
+            ut_bf[h] = grouped
+            turn_pass(ul_bf[h][:], UTB[h], "ut_ps%d" % h, grouped, copy)
+
+        def quantize_listed(h, codes):
+            ut_q[h] = quantize("ut%d" % h, ut_bf[h], P, codes)
 
         ct_bf = [None] * PACK
         corr_rows = [None] * PACK
@@ -296,16 +318,9 @@ def tile_attend_valuepatch_pl_kernel(
                 nc.vector.tensor_copy(out=rows[:, cut:], in_=corr_sb[r][:].indirect(corr_list[:, cut // 16 :]))
             corr_rows[r] = rows
 
-        def turn_corr(r, grouped):
-            turned = bank(("f0", "x0", "f0", "b2")[r], "ct_ps%d" % r, [P, 2, P])
-            words = corr_rows[r].bitcast(F32)
-            for u in range(2):
-                nc.tensor.transpose(turned[:, u, :], words[:, u::2], ident[:])
+        def turn_corr(r, grouped, copy):
             ct_bf[r] = grouped
-            nc.scalar.copy(
-                out=ct_bf[r].bitcast(F32).rearrange("p (m u) -> p m u", u=2),
-                in_=turned[:].rearrange("p u m -> p m u"),
-            )
+            turn_pass(corr_rows[r], CTB[r], "ct_ps%d" % r, grouped, copy)
 
         def quantize_corr(r):
             ct_q[r] = quantize("ct%d" % r, ct_bf[r], P)
@@ -327,29 +342,32 @@ def tile_attend_valuepatch_pl_kernel(
         row_sum(1)
         picked0 = gather_w(0, sbuf("picked0", [P, I], F32, over="corr0")[:])
         weigh(0)
-        turn_corr(0, sbuf("ct_bf0", [P, I], BF16, over="p0")[:])
+        turn_corr(0, sbuf("ct_bf0", [P, I], BF16, over="p0")[:], nc.scalar.copy)
         turn_weights(0)
         copy_weights(0, sbuf("wt_bf0", [P, T], BF16)[:])
-        turn_listed(0, picked0)
         normalise(1)
-        picked1 = gather_w(1, sbuf("picked1", [P, I], F32, over=OVA)[:])
-        gather_corr(1, VECTOR_SLOTS[1], sbuf("rows1", [P, I], BF16, over=OVB)[:])
+        picked1 = gather_w(1, sbuf("picked1", [P, I], F32, over="wf0")[:])
         weigh(1)
         turn_weights(1)
-        copy_weights(1, sbuf("wt_bf1", [P, T], BF16, over=OVC)[:])
+        copy_weights(1, sbuf("wt_bf1", [P, T], BF16)[:])
+        weigh_listed(0, picked0)
+        turn_listed(0, sbuf("ut_bf0", [P, I], BF16)[:], nc.scalar.copy)
+        gather_corr(1, VECTOR_SLOTS[1], sbuf("rows1", [P, I], BF16, over="wf1")[:])
         coarse(0)
-        listed(0)
         quantize_corr(0)
+        weigh_listed(1, picked1)
+        coarse(1)
+        quantize_listed(0, None)
         patch(0, 0)
-        turn_listed(1, picked1)
-        gather_corr(2, VECTOR_SLOTS[2], sbuf("rows2", [P, I], BF16, over="ut_bf0")[:])
-        gather_corr(3, VECTOR_SLOTS[3], sbuf("rows3", [P, I], BF16, over=OVD)[:])
-        after_corr3 = sbuf("after_corr3", [P, 2 * I], BF16, over="corr3")
-        turn_corr(1, after_corr3[:, :I])
-        turn_corr(2, after_corr3[:, I:])
-        turn_corr(3, sbuf("ct_bf3", [P, I], BF16)[:])
-        coarse(1, OVE)
-        listed(1, OVF)
+        gather_corr(2, VECTOR_SLOTS[2], sbuf("rows2", [P, I], BF16, over=OV2)[:])
+        gather_corr(3, VECTOR_SLOTS[3], sbuf("rows3", [P, I], BF16, over="w1")[:])
+        eng = (nc.scalar.copy, nc.vector.tensor_copy)
+        after_corr3 = sbuf("after_corr3", [P, 3 * I], BF16, over="corr3")
+        turn_listed(1, after_corr3[:, :I], eng[ENG[0]])
+        turn_corr(1, after_corr3[:, I : 2 * I], eng[ENG[1]])
+        turn_corr(2, after_corr3[:, 2 * I :], eng[ENG[2]])
+        turn_corr(3, sbuf("ct_bf3", [P, I], BF16)[:], eng[ENG[3]])
+        quantize_listed(1, None)
         patch(0, 1)
         for r in range(1, PACK):
             quantize_corr(r)
@@ -373,7 +391,7 @@ def tile_attend_valuepatch_pl_kernel(
                 scales=o_scales[:, h * P : (h + 1) * P],
                 in_=o_bf[h][:].rearrange("p q r -> p (q r)"),
             )
-        nc.sync.dma_start(
+        nc.scalar.dma_start(
             out=out_1[0].rearrange("p q j -> p (q j)").bitcast(I32), in_=o_codes[:].bitcast(I32)
         )
         for quad in range(4):

from contextlib import ExitStack

import concourse.mybir as mybir
from concourse.masks import make_identity

D, T, I, U, Q, E = 512, 1024, 512, 2048, 256, 512
FLOPS = 2 * D * Q * T + 2 * T * E * Q + 2 * I * E * Q

F32 = mybir.dt.float32
BF16 = mybir.dt.bfloat16
I32 = mybir.dt.int32
U32 = mybir.dt.uint32
U16 = mybir.dt.uint16
U8 = mybir.dt.uint8
FP8X4 = mybir.dt.float8_e4m3fn_x4
ALU = mybir.AluOpType
ACT = mybir.ActivationFunctionType
AXIS_X = mybir.AxisListType.X

P = 128
PACK = 4
K_PASS = P * PACK
HALVES = Q // P
T_PASSES = T // K_PASS
CHUNK = 256
CHUNKS = T // CHUNK
SCALAR_TOKENS = (0, 0, 128, 128)
SCALAR_QUERIES = 0
VECTOR_SLOTS = (0, 0, 512, 128)
OVM = "k_raw2"
OV2 = "wf0"
OVA = "wf0"
OVB = "w0"
OVC = "corr1"
OVD = "wf1"
OVE = "corr2"
OVF = "corr1"
UTB = ("f1", "b3")
CTB = ("f0", "x0", "f0", "x1")
ENG = (1, 0, 1, 0)
LAG = 4
OVER = (None, None, None, None)


def interleave(copy, dst, src):
    copy(
        out=dst.rearrange("p (c i) j -> p c j i", i=4),
        in_=src.rearrange("p j (c i) -> p c j i", i=4),
    )


def tile_attend_valuepatch_pl_kernel(
    tc, query, keys, fac, us, cvals_words, cvals_scales, corr, offs, offs2, out_0, out_1, out_2
):
    nc = tc.nc
    with ExitStack() as ctx:
        lists = ctx.enter_context(tc.tile_pool(name="lists", bufs=1))
        sb = ctx.enter_context(tc.tile_pool(name="sb", bufs=1))
        psum = ctx.enter_context(tc.psum_pool(name="psum", bufs=1))

        def sbuf(name, shape, dtype, over=None):
            return sb.tile(shape, dtype, name=name, tag=over or name, align_bytes=64)

        def bank(tag, name, shape):
            return psum.tile(shape, F32, name=name, tag=tag)

        def quantize(name, grouped, width, codes=None):
            if codes is None:
                codes = sbuf(name + "_codes", [P, width], U32)
            scales = sbuf(name + "_scales", [P, width], U8)
            nc.vector.quantize_mx(out=codes[:].bitcast(FP8X4), scales=scales[:], in_=grouped)
            return codes, scales

        q_raw = sbuf("q_raw", [P, PACK, Q], F32)
        nc.sync.dma_start(out=q_raw[:], in_=query.rearrange("(p j) q -> p j q", j=PACK))
        keys_v = keys.rearrange("(p j) t -> p j t", j=PACK)
        k_raw = []
        for c in range(CHUNKS):
            k_raw.append(sbuf("k_raw%d" % c, [P, PACK, CHUNK], F32))
            nc.sync.dma_start(out=k_raw[c][:], in_=keys_v[:, :, c * CHUNK : (c + 1) * CHUNK])
        cv_raw = sbuf("cv_raw", [P, T_PASSES, E], U32)
        nc.sync.dma_start(
            out=cv_raw[:].bitcast(I32),
            in_=cvals_words.rearrange("z p e j -> p z (e j)").bitcast(I32),
        )
        cs_raw = sbuf("cs_raw", [P, E], U8)
        nc.gpsimd.memset(cs_raw[:].bitcast(I32), 0)
        for quad in range(4):
            nc.scalar.dma_start(
                out=cs_raw[32 * quad : 32 * quad + 4 * T_PASSES, :].bitcast(I32),
                in_=cvals_scales[:, 4 * quad : 4 * quad + 4, :].bitcast(I32),
            )
        fac_col = sbuf("fac_col", [P, T_PASSES, PACK], F32)
        nc.scalar.dma_start(out=fac_col[:], in_=fac[0].rearrange("(z p j) -> p z j", z=T_PASSES, j=PACK))
        corr_v = corr.rearrange("(p r) u -> p r u", r=PACK)
        corr_sb = [sbuf("corr%d" % r, [P, U], F32) for r in range(PACK)]
        nc.sync.dma_start(out=corr_sb[0][:], in_=corr_v[:, 0, :])
        corr_list = lists.tile([P, I // 16], U16, name="corr_list")
        nc.sync.dma_start(corr_list[:], offs2)
        w_list = lists.tile([P, I // 16], U16, name="w_list")
        nc.sync.dma_start(w_list[:], offs)
        us_col = sbuf("us_col", [P, PACK], F32)
        nc.scalar.dma_start(out=us_col[:], in_=us[0].rearrange("(p j) -> p j", j=PACK))
        for r in range(1, PACK):
            nc.sync.dma_start(out=corr_sb[r][:], in_=corr_v[:, r, :])


        ident = sbuf("ident", [P, P], F32)
        make_identity(nc, ident[:])

        def shared_interleave(dst, src, split):
            if split > 0:
                interleave(nc.scalar.copy, dst[:, :split, :], src[:, :, :split])
            if split < dst.shape[1]:
                interleave(nc.vector.tensor_copy, dst[:, split:, :], src[:, :, split:])

        q_bf = sbuf("q_bf", [P, Q, PACK], BF16)
        shared_interleave(q_bf, q_raw, SCALAR_QUERIES)
        q_codes, q_scales = quantize("q", q_bf[:].rearrange("p q j -> p (q j)"), Q)

        neg_max = sbuf("neg_max", [P, HALVES, CHUNKS], F32, over=OVM)
        chunk_sum = sbuf("chunk_sum", [P, HALVES, CHUNKS], F32)
        neg_row_max = sbuf("neg_row_max", [P, HALVES], F32)
        rescale = sbuf("rescale", [P, HALVES, CHUNKS], F32)
        p_sb = [sbuf("p%d" % h, [P, T], F32) for h in range(HALVES)]
        scores = [None] * CHUNKS

        def score(c):
            k_bf = sbuf("k_bf%d" % c, [P, CHUNK, PACK], BF16, over=OVER[c])
            shared_interleave(k_bf, k_raw[c], SCALAR_TOKENS[c])
            k_codes, k_scales = quantize("k%d" % c, k_bf[:].rearrange("p t j -> p (t j)"), CHUNK)
            scores[c] = bank("b%d" % c, "scores%d" % c, [P, HALVES, CHUNK])
            for h in range(HALVES):
                nc.tensor.matmul_mx(
                    out=scores[c][:, h, :],
                    lhsT=q_codes[:, h * P : (h + 1) * P].bitcast(FP8X4),
                    lhsT_scale=q_scales[:, h * P : (h + 1) * P],
                    rhs=k_codes[:].bitcast(FP8X4),
                    rhs_scale=k_scales[:],
                    start=True,
                    stop=True,
                )

        def exponentiate(c):
            nc.vector.tensor_reduce(
                out=neg_max[:, :, c], in_=scores[c][:], axis=AXIS_X, op=ALU.max, negate=True
            )
            if c == CHUNKS - 1:
                nc.vector.tensor_reduce(out=neg_row_max[:], in_=neg_max[:], axis=AXIS_X, op=ALU.min)
            for h in range(HALVES):
                nc.scalar.activation(
                    out=p_sb[h][:, c * CHUNK : (c + 1) * CHUNK],
                    in_=scores[c][:, h, :],
                    func=ACT.Exp,
                    bias=neg_max[:, h, c : c + 1],
                    accum_out=chunk_sum[:, h, c : c + 1],
                )
                if c == CHUNKS - 1:
                    nc.scalar.activation(
                        out=rescale[:, h, :],
                        in_=neg_max[:, h, :],
                        func=ACT.Exp,
                        scale=-1.0,
                        bias=neg_row_max[:, h : h + 1],
                    )

        for c in range(CHUNKS + LAG):
            if c < CHUNKS:
                score(c)
            if c >= LAG:
                exponentiate(c - LAG)

        us_row = bank("b1", "us_row", [P, PACK, P])
        for j in range(PACK):
            nc.tensor.transpose(us_row[:, j, :], us_col[:, j : j + 1].to_broadcast([P, P]), ident[:])
        fac_row = []
        for z in range(T_PASSES):
            fac_row.append(bank("b%d" % (2 + z), "fac_row%d" % z, [P, PACK, P]))
            for j in range(PACK):
                nc.tensor.transpose(fac_row[z][:, j, :], fac_col[:, z, j : j + 1].to_broadcast([P, P]), ident[:])


        cv_codes = sbuf("cv_codes", [P, T_PASSES, E], U32, over="k_bf%d" % (CHUNKS - 1))
        cv_scales = sbuf("cv_scales", [P, E], U8, over="k%d_scales" % (CHUNKS - 1))
        nc.vector.tensor_copy(
            out=cv_codes[:].bitcast(I32).rearrange("p z (r c i) -> p z c r i", r=PACK, i=4),
            in_=cv_raw[:].bitcast(I32).rearrange("p z (c i r) -> p z c r i", r=PACK, i=4),
        )
        nc.vector.tensor_copy(
            out=cv_scales[:].rearrange("p (r c i) -> p c r i", r=PACK, i=16),
            in_=cs_raw[:].rearrange("p (c i r) -> p c r i", r=PACK, i=16),
        )

        w_sb, wf_bf, inv_sum = [None] * HALVES, [None] * HALVES, [None] * HALVES

        def row_sum(h):
            terms = sbuf("terms%d" % h, [P, CHUNKS], F32)
            total = sbuf("total%d" % h, [P, 1], F32)
            nc.vector.scalar_tensor_tensor(
                out=terms[:],
                in0=chunk_sum[:, h, :],
                scalar=1.0,
                in1=rescale[:, h, :],
                op0=ALU.mult,
                op1=ALU.mult,
                accum_out=total[:],
            )
            inv_sum[h] = sbuf("inv_sum%d" % h, [P, 1], F32)
            nc.vector.reciprocal(out=inv_sum[h][:], in_=total[:])

        out_ps = [None, None]
        ut_q = [None, None]
        ct_q = [None] * PACK

        def normalise(h):
            w_sb[h] = sbuf("w%d" % h, [P, T], F32)
            for c in range(CHUNKS):
                cols = slice(c * CHUNK, (c + 1) * CHUNK)
                nc.vector.tensor_scalar(
                    out=w_sb[h][:, cols],
                    in0=p_sb[h][:, cols],
                    scalar1=rescale[:, h, c : c + 1],
                    scalar2=inv_sum[h][:],
                    op0=ALU.mult,
                    op1=ALU.mult,
                )

        def weigh(h):
            wf_bf[h] = sbuf("wf%d" % h, [P, T], BF16)
            for z in range(T_PASSES):
                cols = slice(z * K_PASS, (z + 1) * K_PASS)
                nc.vector.tensor_tensor(
                    out=wf_bf[h][:, cols].rearrange("p (s j) -> p s j", j=PACK),
                    in0=w_sb[h][:, cols].rearrange("p (s j) -> p s j", j=PACK),
                    in1=fac_row[z][:].rearrange("p j s -> p s j"),
                    op=ALU.mult,
                )

        def gather_w(h, picked):
            nc.scalar.activation(out=picked, in_=w_sb[h][:].indirect(w_list[:]), func=ACT.Copy)
            return picked

        wt_bf = [None] * HALVES
        wt_ps = [None] * HALVES

        def turn_weights(h):
            turned = bank("x%d" % h, "wt_ps%d" % h, [P, T_PASSES, 2, P])
            words = wf_bf[h][:].bitcast(F32)
            for z in range(T_PASSES):
                for u in range(2):
                    nc.tensor.transpose(
                        turned[:, z, u, :], words[:, 256 * z + u : 256 * (z + 1) : 2], ident[:]
                    )
            wt_ps[h] = turned

        def copy_weights(h, grouped):
            turned = wt_ps[h]
            wt_bf[h] = grouped
            nc.scalar.copy(
                out=wt_bf[h].bitcast(F32).rearrange("p (z q u) -> p z q u", z=T_PASSES, u=2),
                in_=turned[:].rearrange("p z u q -> p z q u"),
            )

        def coarse(h, codes=None):
            wt_codes, wt_scales = quantize("wt%d" % h, wt_bf[h], T_PASSES * P, codes)
            out_ps[h] = bank(("b0", "b2")[h], "out_ps%d" % h, [P, PACK, P])
            for z in range(T_PASSES):
                for r in range(PACK):
                    nc.tensor.matmul_mx(
                        out=out_ps[h][:, r, :],
                        lhsT=cv_codes[:, z, r * P : (r + 1) * P].bitcast(FP8X4),
                        lhsT_scale=cv_scales[4 * z :, r * P : (r + 1) * P],
                        rhs=wt_codes[:, z * P : (z + 1) * P].bitcast(FP8X4),
                        rhs_scale=wt_scales[:, z * P : (z + 1) * P],
                        start=(z == 0 and r == 0),
                        stop=False,
                    )

        ul_bf = [None] * HALVES
        ut_bf = [None] * HALVES

        def weigh_listed(h, picked):
            ul_bf[h] = sbuf("ul%d" % h, [P, I], BF16)
            nc.vector.tensor_tensor(
                out=ul_bf[h][:].rearrange("p (s j) -> p s j", j=PACK),
                in0=picked.rearrange("p (s j) -> p s j", j=PACK),
                in1=us_row[:].rearrange("p j s -> p s j"),
                op=ALU.mult,
            )

        def turn_pass(rows, tag, name, grouped, copy):
            turned = bank(tag, name, [P, 2, P])
            words = rows.bitcast(F32)
            for u in range(2):
                nc.tensor.transpose(turned[:, u, :], words[:, u::2], ident[:])
            copy(
                out=grouped.bitcast(F32).rearrange("p (m u) -> p m u", u=2),
                in_=turned[:].rearrange("p u m -> p m u"),
            )

        def turn_listed(h, grouped, copy):
            ut_bf[h] = grouped
            turn_pass(ul_bf[h][:], UTB[h], "ut_ps%d" % h, grouped, copy)

        def quantize_listed(h, codes):
            ut_q[h] = quantize("ut%d" % h, ut_bf[h], P, codes)

        ct_bf = [None] * PACK
        corr_rows = [None] * PACK

        def gather_corr(r, vector_share, rows):
            cut = I - vector_share
            if cut:
                nc.scalar.activation(
                    out=rows[:, :cut], in_=corr_sb[r][:].indirect(corr_list[:, : cut // 16]), func=ACT.Copy
                )
            if vector_share:
                nc.vector.tensor_copy(out=rows[:, cut:], in_=corr_sb[r][:].indirect(corr_list[:, cut // 16 :]))
            corr_rows[r] = rows

        def turn_corr(r, grouped, copy):
            ct_bf[r] = grouped
            turn_pass(corr_rows[r], CTB[r], "ct_ps%d" % r, grouped, copy)

        def quantize_corr(r):
            ct_q[r] = quantize("ct%d" % r, ct_bf[r], P)

        def patch(r, h):
            nc.tensor.matmul_mx(
                out=out_ps[h][:, r, :],
                lhsT=ct_q[r][0][:].bitcast(FP8X4),
                lhsT_scale=ct_q[r][1][:],
                rhs=ut_q[h][0][:].bitcast(FP8X4),
                rhs_scale=ut_q[h][1][:],
                start=False,
                stop=(r == PACK - 1),
            )

        row_sum(0)
        gather_corr(0, VECTOR_SLOTS[0], sbuf("rows0", [P, I], BF16, over=OVM or "neg_max")[:])
        normalise(0)
        row_sum(1)
        picked0 = gather_w(0, sbuf("picked0", [P, I], F32, over="corr0")[:])
        weigh(0)
        turn_corr(0, sbuf("ct_bf0", [P, I], BF16, over="p0")[:], nc.scalar.copy)
        turn_weights(0)
        copy_weights(0, sbuf("wt_bf0", [P, T], BF16)[:])
        normalise(1)
        picked1 = gather_w(1, sbuf("picked1", [P, I], F32, over="wf0")[:])
        weigh(1)
        turn_weights(1)
        copy_weights(1, sbuf("wt_bf1", [P, T], BF16)[:])
        weigh_listed(0, picked0)
        turn_listed(0, sbuf("ut_bf0", [P, I], BF16)[:], nc.scalar.copy)
        gather_corr(1, VECTOR_SLOTS[1], sbuf("rows1", [P, I], BF16, over="wf1")[:])
        coarse(0)
        quantize_corr(0)
        weigh_listed(1, picked1)
        coarse(1)
        quantize_listed(0, None)
        patch(0, 0)
        gather_corr(2, VECTOR_SLOTS[2], sbuf("rows2", [P, I], BF16, over=OV2)[:])
        gather_corr(3, VECTOR_SLOTS[3], sbuf("rows3", [P, I], BF16, over="w1")[:])
        eng = (nc.scalar.copy, nc.vector.tensor_copy)
        after_corr3 = sbuf("after_corr3", [P, 3 * I], BF16, over="corr3")
        turn_listed(1, after_corr3[:, :I], eng[ENG[0]])
        turn_corr(1, after_corr3[:, I : 2 * I], eng[ENG[1]])
        turn_corr(2, after_corr3[:, 2 * I :], eng[ENG[2]])
        turn_corr(3, sbuf("ct_bf3", [P, I], BF16)[:], eng[ENG[3]])
        quantize_listed(1, None)
        patch(0, 1)
        for r in range(1, PACK):
            quantize_corr(r)
            for h in range(HALVES):
                patch(r, h)

        out_v = out_0.rearrange("(p r) q -> p r q", r=PACK)
        o_sb = [sbuf("o_sb%d" % h, [P, PACK, P], F32) for h in range(HALVES)]
        o_bf = [sbuf("o_bf%d" % h, [P, P, PACK], BF16) for h in range(HALVES)]
        o_codes = sbuf("o_codes", [P, Q], U32)
        o_scales = sbuf("o_scales", [P, Q], U8)
        nc.vector.tensor_copy(out=o_bf[0][:], in_=out_ps[0][:].rearrange("p r q -> p q r"))
        nc.scalar.copy(out=o_sb[1][:], in_=out_ps[1][:])
        nc.sync.dma_start(out=out_v[:, :, P:], in_=o_sb[1][:])
        nc.scalar.copy(out=o_sb[0][:], in_=out_ps[0][:])
        nc.sync.dma_start(out=out_v[:, :, :P], in_=o_sb[0][:])
        interleave(nc.vector.tensor_copy, o_bf[1][:], o_sb[1][:])
        for h in range(HALVES):
            nc.vector.quantize_mx(
                out=o_codes[:, h * P : (h + 1) * P].bitcast(FP8X4),
                scales=o_scales[:, h * P : (h + 1) * P],
                in_=o_bf[h][:].rearrange("p q r -> p (q r)"),
            )
        nc.scalar.dma_start(
            out=out_1[0].rearrange("p q j -> p (q j)").bitcast(I32), in_=o_codes[:].bitcast(I32)
        )
        for quad in range(4):
            queue = nc.scalar if quad % 2 else nc.sync
            queue.dma_start(
                out=out_2[0][4 * quad : 4 * quad + 4, :].bitcast(I32),
                in_=o_scales[32 * quad : 32 * quad + 4, :].bitcast(I32),
            )
